import numpy as np
import ml_dtypes


def mxq(x, axis, fmt="e4m3"):
    dtype, down = {"e4m3": (ml_dtypes.float8_e4m3fn, 7), "e5m2": (ml_dtypes.float8_e5m2, 14)}[fmt]
    v = np.moveaxis(np.asarray(x, np.float32).astype(ml_dtypes.bfloat16).astype(np.float64), axis, -1)
    blocks = v.reshape(v.shape[:-1] + (-1, 32))
    amax = np.abs(blocks).max(-1, keepdims=True)
    byte = np.maximum(np.where(amax > 0, np.frexp(amax)[1] - 1 + 127, 0) - down, 1)
    scale = np.exp2(byte - 127.0)
    codes = (blocks / scale).astype(np.float32).astype(dtype).astype(np.float64)
    return np.moveaxis((codes * scale).reshape(v.shape), -1, axis)


WIDE = False


def mx_kscale(k):
    if not WIDE:
        return np.ones(k)
    levels = np.array([10, -10, 5, -5, 0])
    if k % 512:
        return np.exp2(np.random.permutation(np.resize(levels, k // 32))).repeat(32)
    a = np.empty((k // 512, 16))
    for p in range(k // 512):
        a[p, :8] = np.random.permutation(np.resize(levels, 8))
        for g in range(8):
            far = levels[np.abs(levels - a[p, g]) >= 10]
            a[p, g + 8] = far[np.random.randint(len(far))]
    return np.exp2(a.ravel()).repeat(32)


def f64(x):
    return np.asarray(x).astype(np.float64)


def striped(idx):
    return np.tile(np.asarray(idx).reshape(-1, 16).T, (8, 1)).astype(np.uint16)


def unstriped(offs):
    return offs[:16].T.reshape(-1).astype(np.int64)


E2M1 = np.array([0.0, 0.5, 1.0, 1.5, 2.0, 3.0, 4.0, 6.0, -0.0, -0.5, -1.0, -1.5, -2.0, -3.0, -4.0, -6.0])


def pack_weight(w, fmt):
    k, n = w.shape
    w = f64(np.asarray(w, np.float32).astype(ml_dtypes.bfloat16)).reshape(k // 32, 32, n)
    amax = np.abs(w).max(1)
    if fmt == "e4m3":
        byte = np.frexp(amax)[1] - 1 + 127 - 7
    else:
        mant, ex = np.frexp(amax / 6.0)
        byte = np.where(mant > 0.5, ex, ex - 1) + 127
    byte = np.clip(np.where(amax > 0, byte, 1), 1, 254)
    scaled = (w * np.exp2(127.0 - byte)[:, None, :]).reshape(k, n).astype(np.float32)
    by_word = np.ascontiguousarray(scaled.reshape(k // 512, 128, 4, n).transpose(0, 1, 3, 2))
    if fmt == "e4m3":
        words = by_word.astype(ml_dtypes.float8_e4m3fn).view(np.uint8)
    else:
        c = by_word.astype(ml_dtypes.float4_e2m1fn).view(np.uint8) & 0xF
        words = (c[..., 0::2] | (c[..., 1::2] << 4)).reshape(k // 512, 128, 2 * n)
    return np.ascontiguousarray(words), np.ascontiguousarray(byte.astype(np.uint8).reshape(k // 512, 16, n))


def unpack_weight(words, scales, fmt):
    g, _, n = scales.shape
    words = np.ascontiguousarray(words).reshape(g, 128, n, -1)
    if fmt == "e4m3":
        vals = words.view(ml_dtypes.float8_e4m3fn).astype(np.float64)
    else:
        nib = np.empty((g, 128, n, 4), np.uint8)
        nib[..., 0::2] = words & 0xF
        nib[..., 1::2] = words >> 4
        vals = E2M1[nib]
    vals = vals * np.repeat(np.exp2(scales.astype(np.float64) - 127.0), 8, axis=1)[..., None]
    return vals.transpose(0, 1, 3, 2).reshape(g * 512, n)


def bf(x):
    return np.asarray(x, np.float32).astype(ml_dtypes.bfloat16)


def planes(Y):
    r, m = Y.shape
    b = f64(bf(Y)).reshape(r // 32, 32, m)
    amax = np.abs(b).max(1)
    byte = np.clip(np.where(amax > 0, np.frexp(amax)[1] - 1 + 127 - 7, 1), 1, 254)
    codes = (b * np.exp2(127.0 - byte)[:, None, :]).reshape(r, m).astype(np.float32).astype(ml_dtypes.float8_e4m3fn).view(np.uint8)
    words = codes.reshape(r // 512, 128, 4, m).transpose(0, 1, 3, 2)
    return np.ascontiguousarray(words), np.ascontiguousarray(byte.astype(np.uint8).reshape(r // 512, 16, m))


D, T, I, Q, E = 512, 2048, 512, 256, 512


def setup_inputs():
    n = np.random.standard_normal
    idx = np.random.permutation(T)[:I]
    fd = mx_kscale(D)
    fi = mx_kscale(I)
    ti = np.ones(T)
    ti[idx] = fi
    keysp = pack_weight(n((D, T)) / fd[:, None], "e2m1")
    return {
        "query": (n((D, Q)) * 0.5 / np.sqrt(D) * fd[:, None]).astype(np.float32),
        "query2": (n((D, Q)) * 0.5 / np.sqrt(D) * fd[:, None]).astype(np.float32),
        "keys_words": keysp[0],
        "keys_scales": keysp[1],
        "share": np.tile(np.random.uniform(0.0, 1.0, T), (128, 1)).astype(np.float32),
        "size": (np.random.uniform(0.5, 2.0, (1, I)) * fi).astype(np.float32),
        "vals": (n((E, T)) / ti).astype(np.float32),
        "offs": striped(idx),
    }


def reference(query, query2, keys_words, keys_scales, share, size, vals, offs):
    idx = unstriped(offs)
    keysu = unpack_weight(keys_words, keys_scales, "e2m1")
    queryq = mxq(f64(query), 0, "e4m3")
    keysidxg = keysu[:, idx]
    a = queryq.T @ keysidxg
    query2q = mxq(f64(query2), 0, "e4m3")
    b = query2q.T @ keysidxg
    s = b + (a - b) * f64(share)[:1][:, idx]
    p = np.exp(s - np.max(s, axis=1, keepdims=True))
    w = p * f64(size) / np.sum(p, axis=1, keepdims=True)
    wt = w.T
    vt = f64(vals)[:, idx].T
    vtq = mxq(vt, 0, "e4m3")
    wtq = mxq(wt, 0, "e4m3")
    o = vtq.T @ wtq
    words, scales = planes(o)
    return o, words, scales

@@ -1,0 +1,259 @@
+from contextlib import ExitStack
+
+import concourse.mybir as mybir
+from concourse.masks import make_identity
+
+D, T, I, Q, E = 512, 2048, 512, 256, 512
+FLOPS = 2 * (2 * D * Q * I + I * E * Q)
+BYTES = 4 * (2 * D * Q + T + I + E * T + E * Q) + D * T // 2 + D * T // 32 + 2 * 128 * I // 16 + E * Q + E * Q // 32
+
+F32 = mybir.dt.float32
+BF16 = mybir.dt.bfloat16
+I32 = mybir.dt.int32
+U32 = mybir.dt.uint32
+U16 = mybir.dt.uint16
+U8 = mybir.dt.uint8
+FP8X4 = mybir.dt.float8_e4m3fn_x4
+FP4X4 = mybir.dt.float4_e2m1fn_x4
+ALU = mybir.AluOpType
+ACT = mybir.ActivationFunctionType
+AXIS = mybir.AxisListType
+
+P = 128
+PACK = 4
+BANK = 512
+HALVES = Q // P
+SHARE_ROW = P - 1
+
+
+def tile_attend_slotmixture_pl_kernel(tc, query, query2, keys_words, keys_scales, share, size, vals, offs, out_0, out_1, out_2):
+    nc = tc.nc
+    with ExitStack() as ctx:
+        sb = ctx.enter_context(tc.tile_pool(name="sb", bufs=1))
+        ps = ctx.enter_context(tc.psum_pool(name="ps", bufs=1))
+
+        def sbuf(name, shape, dtype, tag=None):
+            return sb.tile(shape, dtype, name=name, tag=tag or name, align_bytes=64)
+
+        def bank(index, name):
+            return ps.tile([P, BANK], F32, name=name, tag=f"bank{index}")
+
+        def interleave(copy, dst, src, first, count):
+            copy(
+                out=dst.rearrange("p (c i t) -> p c t i", i=PACK, t=PACK)[:, first : first + count],
+                in_=src.rearrange("p (t c i) -> p c t i", i=PACK, t=PACK)[:, first : first + count],
+            )
+
+        offsets = sbuf("offsets", [P, I // 16], U16)
+        share_pool = sbuf("share_pool", [P, T], F32)
+        kscale_pool = sbuf("kscale_pool", [P, T], U8)
+        kword_pool = sbuf("kword_pool", [P, T], U16)
+        q_raw = [sbuf(f"q_raw{j}", [P, PACK * Q], F32) for j in range(2)]
+        size_col = sbuf("size_col", [P, PACK], F32)
+        val_pool = [sbuf(f"val_pool{t}", [P, T], F32) for t in range(PACK)]
+        ident = sbuf("ident", [P, P], F32)
+        warm = sbuf("warm", [P, 16], F32)
+
+        nc.vector.memset(kscale_pool[:].bitcast(I32), 0)
+        nc.vector.memset(share_pool[0:SHARE_ROW, :].bitcast(I32), 0)
+        nc.gpsimd.memset(warm[:, 0:8], 0.0)
+        make_identity(nc, ident[:])
+        nc.scalar.activation(warm[:, 8:16], warm[:, 0:8], ACT.Exp)
+
+        nc.sync.dma_start(offsets[:], offs)
+        nc.sync.dma_start(out=share_pool[SHARE_ROW:P, :], in_=share[SHARE_ROW:P, :])
+        for quad in range(4):
+            nc.sync.dma_start(
+                out=kscale_pool[32 * quad : 32 * quad + 4, :].bitcast(I32),
+                in_=keys_scales[0, 4 * quad : 4 * quad + 4, :].bitcast(I32),
+            )
+        nc.sync.dma_start(out=q_raw[0][:], in_=query.rearrange("(p t) q -> p (t q)", t=PACK))
+        nc.sync.dma_start(out=kword_pool[:].bitcast(I32), in_=keys_words[0].bitcast(I32))
+        nc.sync.dma_start(out=q_raw[1][:], in_=query2.rearrange("(p t) q -> p (t q)", t=PACK))
+        nc.sync.dma_start(out=size_col[:], in_=size.rearrange("o (p t) -> p (o t)", t=PACK))
+        vals_dealt = vals.rearrange("(p t) c -> t p c", t=PACK)
+        for t in range(PACK):
+            nc.sync.dma_start(out=val_pool[t][:], in_=vals_dealt[t])
+
+        share_g = sbuf("share_g", [P, I], F32)
+        nc.vector.tensor_copy(share_g[:], share_pool[:].indirect(offsets[:]))
+        kscale_g = sbuf("kscale_g", [P, I], U8)
+        nc.vector.tensor_copy(kscale_g[:], kscale_pool[:].indirect(offsets[:]))
+
+        share_ps = bank(6, "share_ps")
+        for c in range(PACK):
+            nc.tensor.transpose(share_ps[:, c * P : (c + 1) * P], share_g[:, c * P : (c + 1) * P], ident[:])
+
+        q_bf = [sbuf(f"q_bf{j}", [P, PACK * Q], BF16) for j in range(2)]
+        q_codes = [sbuf(f"q_codes{j}", [P, Q], U32) for j in range(2)]
+        q_scales = [sbuf(f"q_scales{j}", [P, Q], U8) for j in range(2)]
+        interleave(nc.scalar.copy, q_bf[0][:], q_raw[0][:], 0, 40)
+        interleave(nc.vector.tensor_copy, q_bf[0][:], q_raw[0][:], 40, 24)
+        factor = [sbuf(f"factor{j}", [P, PACK], F32) for j in range(2)]
+        share_cols = share_ps[:, SHARE_ROW:BANK:P]
+        nc.scalar.copy(out=factor[0][:], in_=share_cols)
+        nc.scalar.activation(factor[1][:], share_cols, ACT.Copy, bias=1.0, scale=-1.0)
+        nc.vector.quantize_mx(out=q_codes[0][:].bitcast(FP8X4), scales=q_scales[0][:], in_=q_bf[0][:])
+        kword_g = [sbuf(f"kword_g{g}", [P, I // 2], U16) for g in range(2)]
+        for g in range(2):
+            nc.vector.tensor_copy(kword_g[g][:], kword_pool[:].indirect(offsets[:, 16 * g : 16 * (g + 1)]))
+        interleave(nc.vector.tensor_copy, q_bf[1][:], q_raw[1][:], 0, 64)
+        nc.vector.quantize_mx(out=q_codes[1][:].bitcast(FP8X4), scales=q_scales[1][:], in_=q_bf[1][:])
+
+        ab_ps = [bank(c, f"ab_ps{c}") for c in range(PACK)]
+        part = [[sbuf(f"part{j}_{c}", [P, Q], F32) for c in range(PACK)] for j in range(2)]
+        s_ps = [bank(4 + h, f"s_ps{h}") for h in range(HALVES)]
+        for j in range(2):
+            for c in range(PACK):
+                nc.tensor.matmul_mx(
+                    out=ab_ps[c][:, j * Q : (j + 1) * Q],
+                    lhsT=kword_g[c // 2][:, c % 2 * P : (c % 2 + 1) * P].bitcast(FP4X4),
+                    lhsT_scale=kscale_g[:, c * P : (c + 1) * P],
+                    rhs=q_codes[j][:].bitcast(FP8X4),
+                    rhs_scale=q_scales[j][:],
+                    start=True,
+                    stop=True,
+                )
+            for c in range(PACK):
+                sums = ab_ps[c][:, j * Q : (j + 1) * Q]
+                if j == 1 and c < 2:
+                    nc.vector.scalar_tensor_tensor(part[1][c][:], sums, factor[1][:, c : c + 1], part[0][c][:], ALU.mult, ALU.add)
+                else:
+                    nc.scalar.activation(part[j][c][:], sums, ACT.Copy, scale=factor[j][:, c : c + 1])
+        turns = [(0, 2), (0, 3), (1, 0), (1, 1), (1, 2), (1, 3)]
+        for j, c in turns:
+            for h in range(HALVES):
+                nc.tensor.matmul(
+                    s_ps[h][:, c * P : (c + 1) * P],
+                    part[j][c][:, h * P : (h + 1) * P],
+                    ident[:],
+                    is_transpose=True,
+                    start=((j, c) == turns[0]),
+                    stop=((j, c) == turns[-1]),
+                )
+
+        size_ps = bank(3, "size_ps")
+        for t in range(PACK):
+            nc.tensor.transpose(size_ps[:, t * P : (t + 1) * P], size_col[:, t : t + 1].to_broadcast([P, P]), ident[:])
+        size_row = sbuf("size_row", [P, I], F32)
+        nc.scalar.copy(
+            out=size_row[:].rearrange("p (u s e) -> p u s e", u=2, e=2),
+            in_=size_ps[:].rearrange("p (u e s) -> p u s e", u=2, e=2),
+        )
+        v_codes = [sbuf(f"v_codes{t}", [P, P], U32, tag="val_pool3" if t == 2 else None) for t in range(PACK)]
+        v_scales = [sbuf(f"v_scales{t}", [P, P], U8) for t in range(PACK)]
+        v_g = [sbuf(f"v_g{t}", [P, I], BF16) for t in range(PACK)]
+        v_bf = [sbuf(f"v_bf{t}", [P, PACK * P], BF16) for t in range(PACK)]
+
+        def gather_values(t):
+            nc.vector.tensor_copy(v_g[t][:], val_pool[t][:].indirect(offsets[:]))
+
+        def turn_values(t):
+            turned = bank(6 + t % 2, f"v_ps{t}")
+            words = v_g[t][:].bitcast(F32)
+            for u in range(2):
+                nc.tensor.transpose(turned[:, u * P : (u + 1) * P], words[:, u : 2 * P : 2], ident[:])
+            nc.scalar.copy(
+                out=v_bf[t][:].bitcast(F32).rearrange("p (c u) -> p c u", u=2),
+                in_=turned[:, 0 : 2 * P].rearrange("p (u c) -> p c u", u=2),
+            )
+
+        def quantize_values(t):
+            nc.vector.quantize_mx(out=v_codes[t][:].bitcast(FP8X4), scales=v_scales[t][:], in_=v_bf[t][:])
+
+        gather_values(0)
+        turn_values(0)
+
+        neg_max = sbuf("neg_max", [P, HALVES], F32, tag="val_pool0")
+        row_sum = [sbuf(f"row_sum{h}", [P, 1], F32) for h in range(HALVES)]
+        inv_sum = sbuf("inv_sum", [P, HALVES], F32, tag="val_pool1")
+        p_exp = [sbuf(f"p_exp{h}", [P, I], F32) for h in range(HALVES)]
+        w_row = [sbuf(f"w_row{h}", [P, I], BF16) for h in range(HALVES)]
+        w_bf = [sbuf(f"w_bf{h}", [P, PACK * P], BF16) for h in range(HALVES)]
+        w_codes = sbuf("w_codes", [P, Q], U32, tag="val_pool2")
+        w_scales = [sbuf(f"w_scales{h}", [P, P], U8) for h in range(HALVES)]
+        for h in range(HALVES):
+            nc.vector.tensor_reduce(neg_max[:, h : h + 1], s_ps[h][:], AXIS.X, ALU.max, negate=True)
+            nc.scalar.activation(
+                p_exp[h][:].rearrange("p (u s e) -> p u s e", u=2, e=2),
+                s_ps[h][:].rearrange("p (s u e) -> p u s e", u=2, e=2),
+                ACT.Exp,
+                bias=neg_max[:, h : h + 1],
+                scale=1.0,
+                accum_out=row_sum[h][:],
+            )
+        quantize_values(0)
+        gather_values(1)
+        turn_values(1)
+        for h in range(HALVES):
+            nc.vector.reciprocal(inv_sum[:, h : h + 1], row_sum[h][:])
+        for h in range(HALVES):
+            nc.vector.scalar_tensor_tensor(w_row[h][:], p_exp[h][:], inv_sum[:, h : h + 1], size_row[:], ALU.mult, ALU.mult)
+            turned = bank(h, f"w_ps{h}")
+            words = w_row[h][:].bitcast(F32)
+            for u in range(2):
+                nc.tensor.transpose(turned[:, u * P : (u + 1) * P], words[:, u * P : (u + 1) * P], ident[:])
+            nc.scalar.copy(
+                out=w_bf[h][:].bitcast(F32).rearrange("p (c u) -> p c u", u=2),
+                in_=turned[:, 0 : 2 * P].rearrange("p (u c) -> p c u", u=2),
+            )
+        quantize_values(1)
+        gather_values(2)
+        turn_values(2)
+        for h in range(HALVES):
+            nc.vector.quantize_mx(out=w_codes[:, h * P : (h + 1) * P].bitcast(FP8X4), scales=w_scales[h][:], in_=w_bf[h][:])
+
+        o_ps = [bank(2 + h, f"o_ps{h}") for h in range(HALVES)]
+        o_f32 = [sbuf(f"o_f32_{g}", [P, 2, Q], F32) for g in range(2)]
+        o_bf = [sbuf(f"o_bf{h}", [P, PACK * P], BF16) for h in range(HALVES)]
+        o_codes = sbuf("o_codes", [P, Q], U32)
+        o_scales = sbuf("o_scales", [P, Q], U8)
+        out_dealt = out_0.rearrange("(p t) q -> p t q", t=PACK)
+
+        def multiply_values(t):
+            for h in range(HALVES):
+                nc.tensor.matmul_mx(
+                    out=o_ps[h][:, t * P : (t + 1) * P],
+                    lhsT=v_codes[t][:].bitcast(FP8X4),
+                    lhsT_scale=v_scales[t][:],
+                    rhs=w_codes[:, h * P : (h + 1) * P].bitcast(FP8X4),
+                    rhs_scale=w_scales[h][:],
+                    start=True,
+                    stop=True,
+                )
+
+        def store_pair(g, queue):
+            for h in range(HALVES):
+                nc.scalar.copy(
+                    out=o_f32[g][:, :, h * P : (h + 1) * P],
+                    in_=o_ps[h][:, 2 * g * P : 2 * (g + 1) * P].rearrange("p (t q) -> p t q", t=2),
+                )
+            queue.dma_start(out=out_dealt[:, 2 * g : 2 * g + 2, :], in_=o_f32[g][:])
+
+        multiply_values(0)
+        multiply_values(1)
+        store_pair(0, nc.sync)
+        gather_values(3)
+        turn_values(3)
+        quantize_values(2)
+        multiply_values(2)
+        quantize_values(3)
+        multiply_values(3)
+        for h, copy in enumerate((nc.scalar.copy, nc.vector.tensor_copy)):
+            copy(
+                out=o_bf[h][:].rearrange("p (q t) -> p q t", t=PACK),
+                in_=o_ps[h][:].rearrange("p (t q) -> p q t", t=PACK),
+            )
+        for h in range(HALVES):
+            nc.vector.quantize_mx(
+                out=o_codes[:, h * P : (h + 1) * P].bitcast(FP8X4),
+                scales=o_scales[:, h * P : (h + 1) * P],
+                in_=o_bf[h][:],
+            )
+        store_pair(1, nc.scalar)
+        nc.sync.dma_start(out=out_1[0].rearrange("p c r -> p (c r)").bitcast(I32), in_=o_codes[:].bitcast(I32))
+        for quad in range(4):
+            nc.sync.dma_start(
+                out=out_2[0, 4 * quad : 4 * quad + 4, :].bitcast(I32),
+                in_=o_scales[32 * quad : 32 * quad + 4, :].bitcast(I32),
+            )

@@ -54,23 +54,24 @@ def tile_attend_slotmixture_pl_kernel(tc, query, query2, keys_words, keys_scales
         ident = sbuf("ident", [P, P], F32)
         warm = sbuf("warm", [P, 16], F32)
 
-        nc.vector.memset(kscale_pool[:].bitcast(I32), 0)
-        nc.vector.memset(share_pool[0:SHARE_ROW, :].bitcast(I32), 0)
+        nc.vector.memset(share_pool[0:SHARE_ROW, 0 : T // 2].bitcast(I32), 0)
+        nc.gpsimd.memset(kscale_pool[:].bitcast(I32), 0)
         nc.gpsimd.memset(warm[:, 0:8], 0.0)
+        nc.gpsimd.memset(share_pool[0:SHARE_ROW, T // 2 : T].bitcast(I32), 0)
         make_identity(nc, ident[:])
-        nc.scalar.activation(warm[:, 8:16], warm[:, 0:8], ACT.Exp)
 
         nc.sync.dma_start(offsets[:], offs)
         nc.sync.dma_start(out=share_pool[SHARE_ROW:P, :], in_=share[SHARE_ROW:P, :])
+        nc.sync.dma_start(out=q_raw[0][:], in_=query.rearrange("(p t) q -> p (t q)", t=PACK))
         for quad in range(4):
             nc.sync.dma_start(
                 out=kscale_pool[32 * quad : 32 * quad + 4, :].bitcast(I32),
                 in_=keys_scales[0, 4 * quad : 4 * quad + 4, :].bitcast(I32),
             )
-        nc.sync.dma_start(out=q_raw[0][:], in_=query.rearrange("(p t) q -> p (t q)", t=PACK))
+        nc.scalar.activation(warm[:, 8:16], warm[:, 0:8], ACT.Exp)
         nc.sync.dma_start(out=kword_pool[:].bitcast(I32), in_=keys_words[0].bitcast(I32))
-        nc.sync.dma_start(out=q_raw[1][:], in_=query2.rearrange("(p t) q -> p (t q)", t=PACK))
         nc.sync.dma_start(out=size_col[:], in_=size.rearrange("o (p t) -> p (o t)", t=PACK))
+        nc.sync.dma_start(out=q_raw[1][:], in_=query2.rearrange("(p t) q -> p (t q)", t=PACK))
         vals_dealt = vals.rearrange("(p t) c -> t p c", t=PACK)
         for t in range(PACK):
             nc.sync.dma_start(out=val_pool[t][:], in_=vals_dealt[t])
@@ -87,41 +88,80 @@ def tile_attend_slotmixture_pl_kernel(tc, query, query2, keys_words, keys_scales
         q_bf = [sbuf(f"q_bf{j}", [P, PACK * Q], BF16) for j in range(2)]
         q_codes = [sbuf(f"q_codes{j}", [P, Q], U32) for j in range(2)]
         q_scales = [sbuf(f"q_scales{j}", [P, Q], U8) for j in range(2)]
-        interleave(nc.scalar.copy, q_bf[0][:], q_raw[0][:], 0, 40)
-        interleave(nc.vector.tensor_copy, q_bf[0][:], q_raw[0][:], 40, 24)
-        factor = [sbuf(f"factor{j}", [P, PACK], F32) for j in range(2)]
+        interleave(nc.scalar.copy, q_bf[0][:], q_raw[0][:], 0, 64)
+        factors = sbuf("factors", [P, 2 * PACK], F32, tag="q_raw0")
+        factor = [factors[:, 0:PACK], factors[:, PACK : 2 * PACK]]
         share_cols = share_ps[:, SHARE_ROW:BANK:P]
-        nc.scalar.copy(out=factor[0][:], in_=share_cols)
-        nc.scalar.activation(factor[1][:], share_cols, ACT.Copy, bias=1.0, scale=-1.0)
-        nc.vector.quantize_mx(out=q_codes[0][:].bitcast(FP8X4), scales=q_scales[0][:], in_=q_bf[0][:])
+        nc.scalar.copy(out=factor[0], in_=share_cols)
+        nc.scalar.activation(factor[1], share_cols, ACT.Copy, bias=1.0, scale=-1.0)
+        size_ps = bank(7, "size_ps")
+        for t in range(PACK):
+            nc.tensor.transpose(size_ps[:, t * P : (t + 1) * P], size_col[:, t : t + 1].to_broadcast([P, P]), ident[:])
+        size_row = sbuf("size_row", [P, I], F32)
+        nc.scalar.copy(
+            out=size_row[:].rearrange("p (u s e) -> p u s e", u=2, e=2),
+            in_=size_ps[:].rearrange("p (u e s) -> p u s e", u=2, e=2),
+        )
         kword_g = [sbuf(f"kword_g{g}", [P, I // 2], U16) for g in range(2)]
         for g in range(2):
             nc.vector.tensor_copy(kword_g[g][:], kword_pool[:].indirect(offsets[:, 16 * g : 16 * (g + 1)]))
-        interleave(nc.vector.tensor_copy, q_bf[1][:], q_raw[1][:], 0, 64)
+            if g == 0:
+                nc.vector.quantize_mx(out=q_codes[0][:].bitcast(FP8X4), scales=q_scales[0][:], in_=q_bf[0][:])
+        interleave(nc.scalar.copy, q_bf[1][:], q_raw[1][:], 0, 64)
         nc.vector.quantize_mx(out=q_codes[1][:].bitcast(FP8X4), scales=q_scales[1][:], in_=q_bf[1][:])
 
-        ab_ps = [bank(c, f"ab_ps{c}") for c in range(PACK)]
-        part = [[sbuf(f"part{j}_{c}", [P, Q], F32) for c in range(PACK)] for j in range(2)]
+        first_codes = sbuf("first_codes", [P, 2 * P], U32)
+        late_codes = sbuf("late_codes", [P, 2 * P + Q], U32, tag="val_pool3")
+        v_codes = [first_codes[:], late_codes[:, 0 : 2 * P]]
+        w_codes = late_codes[:, 2 * P : 2 * P + Q]
+        v_scales = [sbuf(f"v_scales{g}", [P, 2 * P], U8) for g in range(2)]
+        v_g = [sbuf(f"v_g{t}", [P, I], BF16) for t in range(PACK)]
+        v_bf = [sbuf(f"v_bf{g}", [P, 2 * PACK * P], BF16) for g in range(2)]
+
+        def gather_values(t):
+            nc.vector.tensor_copy(v_g[t][:], val_pool[t][:].indirect(offsets[:]))
+
+        def turn_values(t):
+            turned = bank(1 + t % 2, f"v_ps{t}")
+            words = v_g[t][:].bitcast(F32)
+            for u in range(2):
+                nc.tensor.transpose(turned[:, u * P : (u + 1) * P], words[:, u : 2 * P : 2], ident[:])
+            nc.scalar.copy(
+                out=v_bf[t // 2][:, t % 2 * I : (t % 2 + 1) * I].bitcast(F32).rearrange("p (c u) -> p c u", u=2),
+                in_=turned[:, 0 : 2 * P].rearrange("p (u c) -> p c u", u=2),
+            )
+
+        def quantize_values(first, count):
+            g, lo, hi = first // 2, first % 2, first % 2 + count
+            nc.vector.quantize_mx(
+                out=v_codes[g][:, lo * P : hi * P].bitcast(FP8X4),
+                scales=v_scales[g][:, lo * P : hi * P],
+                in_=v_bf[g][:, lo * I : hi * I],
+            )
+
+        mixed = sbuf("mixed", [P, 2 * Q], F32, tag="val_pool0")
+        first_parts = sbuf("first_parts", [P, PACK * Q], F32, tag="q_raw1")
+        part = [[first_parts[:, c * Q : (c + 1) * Q] for c in range(PACK)]]
+        part.append([sbuf(f"part1_{c}", [P, Q], F32)[:] for c in range(2)] + [mixed[:, 0:Q], mixed[:, Q : 2 * Q]])
         s_ps = [bank(4 + h, f"s_ps{h}") for h in range(HALVES)]
-        for j in range(2):
-            for c in range(PACK):
-                nc.tensor.matmul_mx(
-                    out=ab_ps[c][:, j * Q : (j + 1) * Q],
-                    lhsT=kword_g[c // 2][:, c % 2 * P : (c % 2 + 1) * P].bitcast(FP4X4),
-                    lhsT_scale=kscale_g[:, c * P : (c + 1) * P],
-                    rhs=q_codes[j][:].bitcast(FP8X4),
-                    rhs_scale=q_scales[j][:],
-                    start=True,
-                    stop=True,
-                )
-            for c in range(PACK):
-                sums = ab_ps[c][:, j * Q : (j + 1) * Q]
-                if j == 1 and c < 2:
-                    nc.vector.scalar_tensor_tensor(part[1][c][:], sums, factor[1][:, c : c + 1], part[0][c][:], ALU.mult, ALU.add)
-                else:
-                    nc.scalar.activation(part[j][c][:], sums, ACT.Copy, scale=factor[j][:, c : c + 1])
-        turns = [(0, 2), (0, 3), (1, 0), (1, 1), (1, 2), (1, 3)]
-        for j, c in turns:
+
+        def score(j, c, out):
+            nc.tensor.matmul_mx(
+                out=out,
+                lhsT=kword_g[c // 2][:, c % 2 * P : (c % 2 + 1) * P].bitcast(FP4X4),
+                lhsT_scale=kscale_g[:, c * P : (c + 1) * P],
+                rhs=q_codes[j][:].bitcast(FP8X4),
+                rhs_scale=q_scales[j][:],
+                start=True,
+                stop=True,
+            )
+
+        def scale(j, c, sums):
+            nc.scalar.activation(part[j][c], sums, ACT.Copy, scale=factor[j][:, c : c + 1])
+
+        turns = [(0, 0), (0, 1), (1, 0), (1, 1), (1, 2), (1, 3)]
+
+        def turn(j, c):
             for h in range(HALVES):
                 nc.tensor.matmul(
                     s_ps[h][:, c * P : (c + 1) * P],
@@ -132,46 +172,34 @@ def tile_attend_slotmixture_pl_kernel(tc, query, query2, keys_words, keys_scales
                     stop=((j, c) == turns[-1]),
                 )
 
-        size_ps = bank(3, "size_ps")
-        for t in range(PACK):
-            nc.tensor.transpose(size_ps[:, t * P : (t + 1) * P], size_col[:, t : t + 1].to_broadcast([P, P]), ident[:])
-        size_row = sbuf("size_row", [P, I], F32)
-        nc.scalar.copy(
-            out=size_row[:].rearrange("p (u s e) -> p u s e", u=2, e=2),
-            in_=size_ps[:].rearrange("p (u e s) -> p u s e", u=2, e=2),
-        )
-        v_codes = [sbuf(f"v_codes{t}", [P, P], U32, tag="val_pool3" if t == 2 else None) for t in range(PACK)]
-        v_scales = [sbuf(f"v_scales{t}", [P, P], U8) for t in range(PACK)]
-        v_g = [sbuf(f"v_g{t}", [P, I], BF16) for t in range(PACK)]
-        v_bf = [sbuf(f"v_bf{t}", [P, PACK * P], BF16) for t in range(PACK)]
-
-        def gather_values(t):
-            nc.vector.tensor_copy(v_g[t][:], val_pool[t][:].indirect(offsets[:]))
-
-        def turn_values(t):
-            turned = bank(6 + t % 2, f"v_ps{t}")
-            words = v_g[t][:].bitcast(F32)
-            for u in range(2):
-                nc.tensor.transpose(turned[:, u * P : (u + 1) * P], words[:, u : 2 * P : 2], ident[:])
-            nc.scalar.copy(
-                out=v_bf[t][:].bitcast(F32).rearrange("p (c u) -> p c u", u=2),
-                in_=turned[:, 0 : 2 * P].rearrange("p (u c) -> p c u", u=2),
-            )
-
-        def quantize_values(t):
-            nc.vector.quantize_mx(out=v_codes[t][:].bitcast(FP8X4), scales=v_scales[t][:], in_=v_bf[t][:])
-
+        a_banks = [bank(b, f"a_ps{b}") for b in range(3)]
+        a_ps = [a_banks[0][:, 0:Q], a_banks[1][:, 0:Q], a_banks[2][:, 0:Q], a_banks[2][:, Q : 2 * Q]]
+        for c in range(PACK):
+            score(0, c, a_ps[c])
+        for c in range(PACK):
+            scale(0, c, a_ps[c])
+        b_ps = [bank(b, f"b_ps{c}")[:, 0:Q] for c, b in enumerate((3, 6, 7, 0))]
+        for c in range(PACK):
+            score(1, c, b_ps[c])
+        for c in range(2):
+            scale(1, c, b_ps[c])
         gather_values(0)
+        for c in range(2, PACK):
+            nc.vector.scalar_tensor_tensor(part[1][c], b_ps[c], factor[1][:, c : c + 1], part[0][c], ALU.mult, ALU.add)
+        for j, c in turns:
+            turn(j, c)
         turn_values(0)
 
-        neg_max = sbuf("neg_max", [P, HALVES], F32, tag="val_pool0")
-        row_sum = [sbuf(f"row_sum{h}", [P, 1], F32) for h in range(HALVES)]
-        inv_sum = sbuf("inv_sum", [P, HALVES], F32, tag="val_pool1")
+        gather_values(1)
+        turn_values(1)
+
+        neg_max = sbuf("neg_max", [P, HALVES], F32, tag="val_pool1")
+        row_sum = sbuf("row_sum", [P, HALVES], F32)
+        inv_sum = sbuf("inv_sum", [P, HALVES], F32, tag="val_pool2")
         p_exp = [sbuf(f"p_exp{h}", [P, I], F32) for h in range(HALVES)]
         w_row = [sbuf(f"w_row{h}", [P, I], BF16) for h in range(HALVES)]
-        w_bf = [sbuf(f"w_bf{h}", [P, PACK * P], BF16) for h in range(HALVES)]
-        w_codes = sbuf("w_codes", [P, Q], U32, tag="val_pool2")
-        w_scales = [sbuf(f"w_scales{h}", [P, P], U8) for h in range(HALVES)]
+        w_bf = sbuf("w_bf", [P, PACK * Q], BF16)
+        w_scales = sbuf("w_scales", [P, Q], U8)
         for h in range(HALVES):
             nc.vector.tensor_reduce(neg_max[:, h : h + 1], s_ps[h][:], AXIS.X, ALU.max, negate=True)
             nc.scalar.activation(
@@ -180,80 +208,81 @@ def tile_attend_slotmixture_pl_kernel(tc, query, query2, keys_words, keys_scales
                 ACT.Exp,
                 bias=neg_max[:, h : h + 1],
                 scale=1.0,
-                accum_out=row_sum[h][:],
+                accum_out=row_sum[:, h : h + 1],
             )
-        quantize_values(0)
-        gather_values(1)
-        turn_values(1)
-        for h in range(HALVES):
-            nc.vector.reciprocal(inv_sum[:, h : h + 1], row_sum[h][:])
+        quantize_values(0, 2)
+        gather_values(2)
+        turn_values(2)
+        nc.vector.reciprocal(inv_sum[:], row_sum[:])
         for h in range(HALVES):
             nc.vector.scalar_tensor_tensor(w_row[h][:], p_exp[h][:], inv_sum[:, h : h + 1], size_row[:], ALU.mult, ALU.mult)
-            turned = bank(h, f"w_ps{h}")
+            turned = bank(6 + h, f"w_ps{h}")
             words = w_row[h][:].bitcast(F32)
             for u in range(2):
                 nc.tensor.transpose(turned[:, u * P : (u + 1) * P], words[:, u * P : (u + 1) * P], ident[:])
             nc.scalar.copy(
-                out=w_bf[h][:].bitcast(F32).rearrange("p (c u) -> p c u", u=2),
+                out=w_bf[:, h * I : (h + 1) * I].bitcast(F32).rearrange("p (c u) -> p c u", u=2),
                 in_=turned[:, 0 : 2 * P].rearrange("p (u c) -> p c u", u=2),
             )
-        quantize_values(1)
-        gather_values(2)
-        turn_values(2)
-        for h in range(HALVES):
-            nc.vector.quantize_mx(out=w_codes[:, h * P : (h + 1) * P].bitcast(FP8X4), scales=w_scales[h][:], in_=w_bf[h][:])
+        gather_values(3)
+        turn_values(3)
+        nc.vector.quantize_mx(out=w_codes.bitcast(FP8X4), scales=w_scales[:], in_=w_bf[:])
+        quantize_values(2, 1)
+        quantize_values(3, 1)
 
-        o_ps = [bank(2 + h, f"o_ps{h}") for h in range(HALVES)]
-        o_f32 = [sbuf(f"o_f32_{g}", [P, 2, Q], F32) for g in range(2)]
-        o_bf = [sbuf(f"o_bf{h}", [P, PACK * P], BF16) for h in range(HALVES)]
+        o_ps = [[bank((3, 0, 4, 5)[2 * g + h], f"o_ps{g}{h}") for h in range(HALVES)] for g in range(2)]
+        o_rows = [sbuf(f"o_rows{g}", [P, 2, Q], F32) for g in range(2)]
+        o_bf = [sbuf(f"o_bf{h}", [P, P, PACK], BF16) for h in range(HALVES)]
         o_codes = sbuf("o_codes", [P, Q], U32)
         o_scales = sbuf("o_scales", [P, Q], U8)
         out_dealt = out_0.rearrange("(p t) q -> p t q", t=PACK)
 
-        def multiply_values(t):
-            for h in range(HALVES):
-                nc.tensor.matmul_mx(
-                    out=o_ps[h][:, t * P : (t + 1) * P],
-                    lhsT=v_codes[t][:].bitcast(FP8X4),
-                    lhsT_scale=v_scales[t][:],
-                    rhs=w_codes[:, h * P : (h + 1) * P].bitcast(FP8X4),
-                    rhs_scale=w_scales[h][:],
-                    start=True,
-                    stop=True,
-                )
-
-        def store_pair(g, queue):
-            for h in range(HALVES):
-                nc.scalar.copy(
-                    out=o_f32[g][:, :, h * P : (h + 1) * P],
-                    in_=o_ps[h][:, 2 * g * P : 2 * (g + 1) * P].rearrange("p (t q) -> p t q", t=2),
-                )
-            queue.dma_start(out=out_dealt[:, 2 * g : 2 * g + 2, :], in_=o_f32[g][:])
-
-        multiply_values(0)
-        multiply_values(1)
-        store_pair(0, nc.sync)
-        gather_values(3)
-        turn_values(3)
-        quantize_values(2)
-        multiply_values(2)
-        quantize_values(3)
-        multiply_values(3)
-        for h, copy in enumerate((nc.scalar.copy, nc.vector.tensor_copy)):
-            copy(
-                out=o_bf[h][:].rearrange("p (q t) -> p q t", t=PACK),
-                in_=o_ps[h][:].rearrange("p (t q) -> p q t", t=PACK),
+        def multiply(t, h):
+            g, e = t // 2, t % 2
+            nc.tensor.matmul_mx(
+                out=o_ps[g][h][:, e * P : (e + 1) * P],
+                lhsT=v_codes[g][:, e * P : (e + 1) * P].bitcast(FP8X4),
+                lhsT_scale=v_scales[g][:, e * P : (e + 1) * P],
+                rhs=w_codes[:, h * P : (h + 1) * P].bitcast(FP8X4),
+                rhs_scale=w_scales[:, h * P : (h + 1) * P],
+                start=True,
+                stop=True,
             )
+
+        def copy_rows(g, h):
+            nc.scalar.copy(
+                out=o_rows[g][:, :, h * P : (h + 1) * P],
+                in_=o_ps[g][h][:, 0 : 2 * P].rearrange("p (e q) -> p e q", e=2),
+            )
+
+        def round_pairs(copy, g, h):
+            copy(
+                out=o_bf[h][:, :, 2 * g : 2 * g + 2],
+                in_=o_ps[g][h][:, 0 : 2 * P].rearrange("p (e q) -> p q e", e=2),
+            )
+
+        for t, h in ((0, 0), (1, 0), (0, 1), (1, 1), (2, 0), (2, 1), (3, 0), (3, 1)):
+            multiply(t, h)
+        copy_rows(0, 0)
+        round_pairs(nc.vector.tensor_copy, 0, 1)
+        copy_rows(0, 1)
+        round_pairs(nc.vector.tensor_copy, 0, 0)
+        nc.sync.dma_start(out=out_dealt[:, 0:2, :], in_=o_rows[0][:])
+        round_pairs(nc.scalar.copy, 1, 0)
+        round_pairs(nc.vector.tensor_copy, 1, 1)
         for h in range(HALVES):
             nc.vector.quantize_mx(
                 out=o_codes[:, h * P : (h + 1) * P].bitcast(FP8X4),
                 scales=o_scales[:, h * P : (h + 1) * P],
-                in_=o_bf[h][:],
+                in_=o_bf[h][:].rearrange("p q t -> p (q t)"),
             )
-        store_pair(1, nc.scalar)
+        for h in range(HALVES):
+            copy_rows(1, h)
+        nc.scalar.dma_start(out=out_dealt[:, 2:4, :], in_=o_rows[1][:])
         nc.sync.dma_start(out=out_1[0].rearrange("p c r -> p (c r)").bitcast(I32), in_=o_codes[:].bitcast(I32))
         for quad in range(4):
-            nc.sync.dma_start(
+            queue = nc.sync if quad < 3 else nc.scalar
+            queue.dma_start(
                 out=out_2[0, 4 * quad : 4 * quad + 4, :].bitcast(I32),
                 in_=o_scales[32 * quad : 32 * quad + 4, :].bitcast(I32),
             )

@@ -20,13 +20,21 @@ ACT = mybir.ActivationFunctionType
 AXIS = mybir.AxisListType
 
 P = 128
-PACK = 4
+PLACES = 4
 BANK = 512
+QUADRANTS = 4
+SLOT_TILES = I // P
 HALVES = Q // P
+LIST_COLUMNS = I // 16
 SHARE_ROW = P - 1
+RUN = 4
+SUMMED_BY_TENSOR = (0, 1)
+SUMMED_BY_VECTOR = (2, 3)
 
 
-def tile_attend_slotmixture_pl_kernel(tc, query, query2, keys_words, keys_scales, share, size, vals, offs, out_0, out_1, out_2):
+def tile_attend_slotmixture_pl_kernel(
+    tc, query, query2, keys_words, keys_scales, share, size, vals, offs, out_0, out_1, out_2
+):
     nc = tc.nc
     with ExitStack() as ctx:
         sb = ctx.enter_context(tc.tile_pool(name="sb", bufs=1))
@@ -38,118 +46,120 @@ def tile_attend_slotmixture_pl_kernel(tc, query, query2, keys_words, keys_scales
         def bank(index, name):
             return ps.tile([P, BANK], F32, name=name, tag=f"bank{index}")
 
-        def interleave(copy, dst, src, first, count):
-            copy(
-                out=dst.rearrange("p (c i t) -> p c t i", i=PACK, t=PACK)[:, first : first + count],
-                in_=src.rearrange("p (t c i) -> p c t i", i=PACK, t=PACK)[:, first : first + count],
-            )
+        def columns(j, width):
+            return slice(j * width, (j + 1) * width)
 
-        offsets = sbuf("offsets", [P, I // 16], U16)
+        def quantize(codes, scales, values):
+            nc.vector.quantize_mx(out=codes.bitcast(FP8X4), scales=scales, in_=values)
+
+        offsets = sbuf("offsets", [P, LIST_COLUMNS], U16)
         share_pool = sbuf("share_pool", [P, T], F32)
-        kscale_pool = sbuf("kscale_pool", [P, T], U8)
-        kword_pool = sbuf("kword_pool", [P, T], U16)
-        q_raw = [sbuf(f"q_raw{j}", [P, PACK * Q], F32) for j in range(2)]
-        size_col = sbuf("size_col", [P, PACK], F32)
-        val_pool = [sbuf(f"val_pool{t}", [P, T], F32) for t in range(PACK)]
+        key_scale_pool = sbuf("key_scale_pool", [P, T], U8)
+        key_word_pool = sbuf("key_word_pool", [P, T], U16)
+        q_raw = [sbuf(f"q_raw{j}", [P, PLACES * Q], F32) for j in range(2)]
+        size_cols = sbuf("size_cols", [P, PLACES], F32)
+        val_pool = [sbuf(f"val_pool{t}", [P, T], F32) for t in range(PLACES)]
         ident = sbuf("ident", [P, P], F32)
-        warm = sbuf("warm", [P, 16], F32)
+        zero = sbuf("zero", [P, 1], F32)
+        one = sbuf("one", [P, 1], F32)
 
         nc.vector.memset(share_pool[0:SHARE_ROW, 0 : T // 2].bitcast(I32), 0)
-        nc.gpsimd.memset(kscale_pool[:].bitcast(I32), 0)
-        nc.gpsimd.memset(warm[:, 0:8], 0.0)
+        nc.gpsimd.memset(key_scale_pool[:].bitcast(I32), 0)
+        nc.gpsimd.memset(zero[:], 0.0)
         nc.gpsimd.memset(share_pool[0:SHARE_ROW, T // 2 : T].bitcast(I32), 0)
         make_identity(nc, ident[:])
 
         nc.sync.dma_start(offsets[:], offs)
         nc.sync.dma_start(out=share_pool[SHARE_ROW:P, :], in_=share[SHARE_ROW:P, :])
-        nc.sync.dma_start(out=q_raw[0][:], in_=query.rearrange("(p t) q -> p (t q)", t=PACK))
-        for quad in range(4):
+        nc.sync.dma_start(out=q_raw[0][:], in_=query.rearrange("(p t) q -> p (t q)", t=PLACES))
+        for quad in range(QUADRANTS):
             nc.sync.dma_start(
-                out=kscale_pool[32 * quad : 32 * quad + 4, :].bitcast(I32),
-                in_=keys_scales[0, 4 * quad : 4 * quad + 4, :].bitcast(I32),
+                out=key_scale_pool[32 * quad : 32 * quad + 4, :].bitcast(I32),
+                in_=keys_scales[0, columns(quad, 4), :].bitcast(I32),
             )
-        nc.scalar.activation(warm[:, 8:16], warm[:, 0:8], ACT.Exp)
-        nc.sync.dma_start(out=kword_pool[:].bitcast(I32), in_=keys_words[0].bitcast(I32))
-        nc.sync.dma_start(out=size_col[:], in_=size.rearrange("o (p t) -> p (o t)", t=PACK))
-        nc.sync.dma_start(out=q_raw[1][:], in_=query2.rearrange("(p t) q -> p (t q)", t=PACK))
-        vals_dealt = vals.rearrange("(p t) c -> t p c", t=PACK)
-        for t in range(PACK):
-            nc.sync.dma_start(out=val_pool[t][:], in_=vals_dealt[t])
+        nc.scalar.activation(one[:], zero[:], ACT.Exp)
+        nc.sync.dma_start(out=key_word_pool[:].bitcast(I32), in_=keys_words[0].bitcast(I32))
+        nc.sync.dma_start(out=size_cols[:], in_=size.rearrange("o (p t) -> p (o t)", t=PLACES))
+        nc.sync.dma_start(out=q_raw[1][:], in_=query2.rearrange("(p t) q -> p (t q)", t=PLACES))
+        vals_by_place = vals.rearrange("(p t) c -> t p c", t=PLACES)
+        for t in range(PLACES):
+            nc.sync.dma_start(out=val_pool[t][:], in_=vals_by_place[t])
 
-        share_g = sbuf("share_g", [P, I], F32)
-        nc.vector.tensor_copy(share_g[:], share_pool[:].indirect(offsets[:]))
-        kscale_g = sbuf("kscale_g", [P, I], U8)
-        nc.vector.tensor_copy(kscale_g[:], kscale_pool[:].indirect(offsets[:]))
+        share_listed = sbuf("share_listed", [P, I], F32)
+        nc.vector.tensor_copy(share_listed[:], share_pool[:].indirect(offsets[:]))
+        key_scales = sbuf("key_scales", [P, I], U8)
+        nc.vector.tensor_copy(key_scales[:], key_scale_pool[:].indirect(offsets[:]))
 
         share_ps = bank(6, "share_ps")
-        for c in range(PACK):
-            nc.tensor.transpose(share_ps[:, c * P : (c + 1) * P], share_g[:, c * P : (c + 1) * P], ident[:])
+        for c in range(SLOT_TILES):
+            nc.tensor.transpose(share_ps[:, columns(c, P)], share_listed[:, columns(c, P)], ident[:])
 
-        q_bf = [sbuf(f"q_bf{j}", [P, PACK * Q], BF16) for j in range(2)]
+        q_bf = [sbuf(f"q_bf{j}", [P, PLACES * Q], BF16) for j in range(2)]
         q_codes = [sbuf(f"q_codes{j}", [P, Q], U32) for j in range(2)]
         q_scales = [sbuf(f"q_scales{j}", [P, Q], U8) for j in range(2)]
-        interleave(nc.scalar.copy, q_bf[0][:], q_raw[0][:], 0, 64)
-        factors = sbuf("factors", [P, 2 * PACK], F32, tag="q_raw0")
-        factor = [factors[:, 0:PACK], factors[:, PACK : 2 * PACK]]
+
+        def interleave_query(j):
+            nc.scalar.copy(
+                out=q_bf[j][:].rearrange("p (c r t) -> p c t r", r=RUN, t=PLACES),
+                in_=q_raw[j][:].rearrange("p (t c r) -> p c t r", r=RUN, t=PLACES),
+            )
+
+        interleave_query(0)
+        factors = sbuf("factors", [P, 2 * SLOT_TILES], F32, tag="q_raw0")
+        factor = [factors[:, columns(j, SLOT_TILES)] for j in range(2)]
         share_cols = share_ps[:, SHARE_ROW:BANK:P]
         nc.scalar.copy(out=factor[0], in_=share_cols)
-        nc.scalar.activation(factor[1], share_cols, ACT.Copy, bias=1.0, scale=-1.0)
-        size_ps = bank(7, "size_ps")
-        for t in range(PACK):
-            nc.tensor.transpose(size_ps[:, t * P : (t + 1) * P], size_col[:, t : t + 1].to_broadcast([P, P]), ident[:])
-        size_row = sbuf("size_row", [P, I], F32)
-        nc.scalar.copy(
-            out=size_row[:].rearrange("p (u s e) -> p u s e", u=2, e=2),
-            in_=size_ps[:].rearrange("p (u e s) -> p u s e", u=2, e=2),
-        )
-        kword_g = [sbuf(f"kword_g{g}", [P, I // 2], U16) for g in range(2)]
-        for g in range(2):
-            nc.vector.tensor_copy(kword_g[g][:], kword_pool[:].indirect(offsets[:, 16 * g : 16 * (g + 1)]))
-            if g == 0:
-                nc.vector.quantize_mx(out=q_codes[0][:].bitcast(FP8X4), scales=q_scales[0][:], in_=q_bf[0][:])
-        interleave(nc.scalar.copy, q_bf[1][:], q_raw[1][:], 0, 64)
-        nc.vector.quantize_mx(out=q_codes[1][:].bitcast(FP8X4), scales=q_scales[1][:], in_=q_bf[1][:])
+        nc.scalar.activation(factor[1], share_cols, ACT.Identity, bias=one[:], scale=-1.0)
 
-        first_codes = sbuf("first_codes", [P, 2 * P], U32)
-        late_codes = sbuf("late_codes", [P, 2 * P + Q], U32, tag="val_pool3")
-        v_codes = [first_codes[:], late_codes[:, 0 : 2 * P]]
-        w_codes = late_codes[:, 2 * P : 2 * P + Q]
+        size_ps = bank(7, "size_ps")
+        for t in range(PLACES):
+            u, e = divmod(t, 2)
+            nc.tensor.transpose(
+                size_ps[:, u * 2 * P + e : (u + 1) * 2 * P : 2], size_cols[:, t : t + 1].to_broadcast([P, P]), ident[:]
+            )
+
+        key_words = [sbuf(f"key_words{g}", [P, I // 2], U16) for g in range(2)]
+
+        def gather_key_words(g):
+            nc.vector.tensor_copy(key_words[g][:], key_word_pool[:].indirect(offsets[:, columns(g, LIST_COLUMNS // 2)]))
+
+        gather_key_words(0)
+        quantize(q_codes[0][:], q_scales[0][:], q_bf[0][:])
+        gather_key_words(1)
+        interleave_query(1)
+        quantize(q_codes[1][:], q_scales[1][:], q_bf[1][:])
+
+        product_codes = sbuf("product_codes", [P, E + Q], U32, tag="val_pool3")
+        v_codes = [product_codes[:, columns(g, 2 * P)] for g in range(2)]
+        w_codes = product_codes[:, E : E + Q]
         v_scales = [sbuf(f"v_scales{g}", [P, 2 * P], U8) for g in range(2)]
-        v_g = [sbuf(f"v_g{t}", [P, I], BF16) for t in range(PACK)]
-        v_bf = [sbuf(f"v_bf{g}", [P, 2 * PACK * P], BF16) for g in range(2)]
+        v_listed = [sbuf(f"v_listed{t}", [P, I], BF16) for t in range(PLACES)]
 
         def gather_values(t):
-            nc.vector.tensor_copy(v_g[t][:], val_pool[t][:].indirect(offsets[:]))
+            nc.vector.tensor_copy(v_listed[t][:], val_pool[t][:].indirect(offsets[:]))
 
-        def turn_values(t):
-            turned = bank(1 + t % 2, f"v_ps{t}")
-            words = v_g[t][:].bitcast(F32)
+        def turn_words(turned, runs, dst):
             for u in range(2):
-                nc.tensor.transpose(turned[:, u * P : (u + 1) * P], words[:, u : 2 * P : 2], ident[:])
+                nc.tensor.transpose(turned[:, columns(u, P)], runs[u], ident[:])
             nc.scalar.copy(
-                out=v_bf[t // 2][:, t % 2 * I : (t % 2 + 1) * I].bitcast(F32).rearrange("p (c u) -> p c u", u=2),
+                out=dst.bitcast(F32).rearrange("p (c u) -> p c u", u=2),
                 in_=turned[:, 0 : 2 * P].rearrange("p (u c) -> p c u", u=2),
             )
 
-        def quantize_values(first, count):
-            g, lo, hi = first // 2, first % 2, first % 2 + count
-            nc.vector.quantize_mx(
-                out=v_codes[g][:, lo * P : hi * P].bitcast(FP8X4),
-                scales=v_scales[g][:, lo * P : hi * P],
-                in_=v_bf[g][:, lo * I : hi * I],
-            )
-
-        mixed = sbuf("mixed", [P, 2 * Q], F32, tag="val_pool0")
-        first_parts = sbuf("first_parts", [P, PACK * Q], F32, tag="q_raw1")
-        part = [[first_parts[:, c * Q : (c + 1) * Q] for c in range(PACK)]]
-        part.append([sbuf(f"part1_{c}", [P, Q], F32)[:] for c in range(2)] + [mixed[:, 0:Q], mixed[:, Q : 2 * Q]])
+        summed = sbuf("summed", [P, len(SUMMED_BY_VECTOR) * Q], F32, tag="val_pool0")
+        a_scaled = sbuf("a_scaled", [P, SLOT_TILES * Q], F32, tag="q_raw1")
+        part = {(0, c): a_scaled[:, columns(c, Q)] for c in range(SLOT_TILES)}
+        for c in SUMMED_BY_TENSOR:
+            part[1, c] = sbuf(f"b_scaled{c}", [P, Q], F32)[:]
+        for n, c in enumerate(SUMMED_BY_VECTOR):
+            part[1, c] = summed[:, columns(n, Q)]
         s_ps = [bank(4 + h, f"s_ps{h}") for h in range(HALVES)]
 
         def score(j, c, out):
             nc.tensor.matmul_mx(
                 out=out,
-                lhsT=kword_g[c // 2][:, c % 2 * P : (c % 2 + 1) * P].bitcast(FP4X4),
-                lhsT_scale=kscale_g[:, c * P : (c + 1) * P],
+                lhsT=key_words[c // 2][:, columns(c % 2, P)].bitcast(FP4X4),
+                lhsT_scale=key_scales[:, columns(c, P)],
                 rhs=q_codes[j][:].bitcast(FP8X4),
                 rhs_scale=q_scales[j][:],
                 start=True,
@@ -157,48 +167,44 @@ def tile_attend_slotmixture_pl_kernel(tc, query, query2, keys_words, keys_scales
             )
 
         def scale(j, c, sums):
-            nc.scalar.activation(part[j][c], sums, ACT.Copy, scale=factor[j][:, c : c + 1])
+            nc.scalar.activation(part[j, c], sums, ACT.Copy, scale=factor[j][:, c : c + 1])
 
-        turns = [(0, 0), (0, 1), (1, 0), (1, 1), (1, 2), (1, 3)]
+        a_banks = [bank(b, f"a_ps{b}") for b in (0, 1, 2)]
+        a_ps = [a_banks[0][:, 0:Q], a_banks[1][:, 0:Q], a_banks[2][:, 0:Q], a_banks[2][:, Q : 2 * Q]]
+        for c in range(SLOT_TILES):
+            score(0, c, a_ps[c])
+        for c in range(SLOT_TILES):
+            scale(0, c, a_ps[c])
+        b_banks = [bank(b, f"b_ps{b}") for b in (3, 6, 0)]
+        b_ps = [b_banks[2][:, 0:Q], b_banks[2][:, Q : 2 * Q], b_banks[0][:, 0:Q], b_banks[1][:, 0:Q]]
+        for c in SUMMED_BY_VECTOR + SUMMED_BY_TENSOR:
+            score(1, c, b_ps[c])
+        for c in SUMMED_BY_TENSOR:
+            scale(1, c, b_ps[c])
+        gather_values(0)
+        for c in SUMMED_BY_VECTOR:
+            nc.vector.scalar_tensor_tensor(part[1, c], b_ps[c], factor[1][:, c : c + 1], part[0, c], ALU.mult, ALU.add)
 
-        def turn(j, c):
+        turns = [(0, c) for c in SUMMED_BY_TENSOR] + [(1, c) for c in range(SLOT_TILES)]
+        for j, c in turns:
             for h in range(HALVES):
                 nc.tensor.matmul(
-                    s_ps[h][:, c * P : (c + 1) * P],
-                    part[j][c][:, h * P : (h + 1) * P],
+                    s_ps[h][:, columns(c, P)],
+                    part[j, c][:, columns(h, P)],
                     ident[:],
                     is_transpose=True,
                     start=((j, c) == turns[0]),
                     stop=((j, c) == turns[-1]),
                 )
 
-        a_banks = [bank(b, f"a_ps{b}") for b in range(3)]
-        a_ps = [a_banks[0][:, 0:Q], a_banks[1][:, 0:Q], a_banks[2][:, 0:Q], a_banks[2][:, Q : 2 * Q]]
-        for c in range(PACK):
-            score(0, c, a_ps[c])
-        for c in range(PACK):
-            scale(0, c, a_ps[c])
-        b_ps = [bank(b, f"b_ps{c}")[:, 0:Q] for c, b in enumerate((3, 6, 7, 0))]
-        for c in range(PACK):
-            score(1, c, b_ps[c])
-        for c in range(2):
-            scale(1, c, b_ps[c])
-        gather_values(0)
-        for c in range(2, PACK):
-            nc.vector.scalar_tensor_tensor(part[1][c], b_ps[c], factor[1][:, c : c + 1], part[0][c], ALU.mult, ALU.add)
-        for j, c in turns:
-            turn(j, c)
-        turn_values(0)
-
         gather_values(1)
-        turn_values(1)
 
         neg_max = sbuf("neg_max", [P, HALVES], F32, tag="val_pool1")
         row_sum = sbuf("row_sum", [P, HALVES], F32)
         inv_sum = sbuf("inv_sum", [P, HALVES], F32, tag="val_pool2")
         p_exp = [sbuf(f"p_exp{h}", [P, I], F32) for h in range(HALVES)]
-        w_row = [sbuf(f"w_row{h}", [P, I], BF16) for h in range(HALVES)]
-        w_bf = sbuf("w_bf", [P, PACK * Q], BF16)
+        w_rows = [sbuf(f"w_rows{h}", [P, I], BF16) for h in range(HALVES)]
+        w_bf = sbuf("w_bf", [P, PLACES * Q], BF16)
         w_scales = sbuf("w_scales", [P, Q], U8)
         for h in range(HALVES):
             nc.vector.tensor_reduce(neg_max[:, h : h + 1], s_ps[h][:], AXIS.X, ALU.max, negate=True)
@@ -210,79 +216,85 @@ def tile_attend_slotmixture_pl_kernel(tc, query, query2, keys_words, keys_scales
                 scale=1.0,
                 accum_out=row_sum[:, h : h + 1],
             )
-        quantize_values(0, 2)
+
+        v_bf = [sbuf("v_bf0", [P, 2 * I], BF16, tag="val_pool1"), sbuf("v_bf1", [P, 2 * I], BF16)]
+
+        def turn_values(t):
+            words = v_listed[t][:].bitcast(F32)
+            runs = [words[:, u : 2 * P : 2] for u in range(2)]
+            turn_words(bank(t % 2, f"v_ps{t}"), runs, v_bf[t // 2][:, columns(t % 2, I)])
+
+        turn_values(0)
+        turn_values(1)
         gather_values(2)
         turn_values(2)
         nc.vector.reciprocal(inv_sum[:], row_sum[:])
-        for h in range(HALVES):
-            nc.vector.scalar_tensor_tensor(w_row[h][:], p_exp[h][:], inv_sum[:, h : h + 1], size_row[:], ALU.mult, ALU.mult)
-            turned = bank(6 + h, f"w_ps{h}")
-            words = w_row[h][:].bitcast(F32)
-            for u in range(2):
-                nc.tensor.transpose(turned[:, u * P : (u + 1) * P], words[:, u * P : (u + 1) * P], ident[:])
-            nc.scalar.copy(
-                out=w_bf[:, h * I : (h + 1) * I].bitcast(F32).rearrange("p (c u) -> p c u", u=2),
-                in_=turned[:, 0 : 2 * P].rearrange("p (u c) -> p c u", u=2),
-            )
+        for h, free_bank in enumerate((6, 3)):
+            nc.vector.scalar_tensor_tensor(w_rows[h][:], p_exp[h][:], inv_sum[:, h : h + 1], size_ps[:], ALU.mult, ALU.mult)
+            words = w_rows[h][:].bitcast(F32)
+            runs = [words[:, columns(u, P)] for u in range(2)]
+            turn_words(bank(free_bank, f"w_ps{h}"), runs, w_bf[:, columns(h, I)])
         gather_values(3)
         turn_values(3)
-        nc.vector.quantize_mx(out=w_codes.bitcast(FP8X4), scales=w_scales[:], in_=w_bf[:])
-        quantize_values(2, 1)
-        quantize_values(3, 1)
+        quantize(w_codes, w_scales[:], w_bf[:])
+        quantize(v_codes[0], v_scales[0][:], v_bf[0][:])
+        for e in range(2):
+            quantize(v_codes[1][:, columns(e, P)], v_scales[1][:, columns(e, P)], v_bf[1][:, columns(e, I)])
 
-        o_ps = [[bank((3, 0, 4, 5)[2 * g + h], f"o_ps{g}{h}") for h in range(HALVES)] for g in range(2)]
+        o_ps = [[bank(b, f"o_ps{b}") for b in free_banks] for free_banks in ((2, 6), (4, 5))]
         o_rows = [sbuf(f"o_rows{g}", [P, 2, Q], F32) for g in range(2)]
-        o_bf = [sbuf(f"o_bf{h}", [P, P, PACK], BF16) for h in range(HALVES)]
+        o_bf = [sbuf(f"o_bf{h}", [P, P, PLACES], BF16) for h in range(HALVES)]
         o_codes = sbuf("o_codes", [P, Q], U32)
         o_scales = sbuf("o_scales", [P, Q], U8)
-        out_dealt = out_0.rearrange("(p t) q -> p t q", t=PACK)
+        out_by_place = out_0.rearrange("(p t) q -> p t q", t=PLACES)
 
-        def multiply(t, h):
-            g, e = t // 2, t % 2
+        def multiply(g, e, h):
             nc.tensor.matmul_mx(
-                out=o_ps[g][h][:, e * P : (e + 1) * P],
-                lhsT=v_codes[g][:, e * P : (e + 1) * P].bitcast(FP8X4),
-                lhsT_scale=v_scales[g][:, e * P : (e + 1) * P],
-                rhs=w_codes[:, h * P : (h + 1) * P].bitcast(FP8X4),
-                rhs_scale=w_scales[:, h * P : (h + 1) * P],
+                out=o_ps[g][h][:, columns(e, P)],
+                lhsT=v_codes[g][:, columns(e, P)].bitcast(FP8X4),
+                lhsT_scale=v_scales[g][:, columns(e, P)],
+                rhs=w_codes[:, columns(h, P)].bitcast(FP8X4),
+                rhs_scale=w_scales[:, columns(h, P)],
                 start=True,
                 stop=True,
             )
 
         def copy_rows(g, h):
             nc.scalar.copy(
-                out=o_rows[g][:, :, h * P : (h + 1) * P],
+                out=o_rows[g][:, :, columns(h, P)],
                 in_=o_ps[g][h][:, 0 : 2 * P].rearrange("p (e q) -> p e q", e=2),
             )
 
-        def round_pairs(copy, g, h):
+        def round_pair(copy, g, h):
             copy(
-                out=o_bf[h][:, :, 2 * g : 2 * g + 2],
+                out=o_bf[h][:, :, columns(g, 2)],
                 in_=o_ps[g][h][:, 0 : 2 * P].rearrange("p (e q) -> p q e", e=2),
             )
 
-        for t, h in ((0, 0), (1, 0), (0, 1), (1, 1), (2, 0), (2, 1), (3, 0), (3, 1)):
-            multiply(t, h)
-        copy_rows(0, 0)
-        round_pairs(nc.vector.tensor_copy, 0, 1)
-        copy_rows(0, 1)
-        round_pairs(nc.vector.tensor_copy, 0, 0)
-        nc.sync.dma_start(out=out_dealt[:, 0:2, :], in_=o_rows[0][:])
-        round_pairs(nc.scalar.copy, 1, 0)
-        round_pairs(nc.vector.tensor_copy, 1, 1)
         for h in range(HALVES):
-            nc.vector.quantize_mx(
-                out=o_codes[:, h * P : (h + 1) * P].bitcast(FP8X4),
-                scales=o_scales[:, h * P : (h + 1) * P],
-                in_=o_bf[h][:].rearrange("p q t -> p (q t)"),
-            )
+            for e in range(2):
+                multiply(0, e, h)
+        for e in range(2):
+            for h in range(HALVES):
+                multiply(1, e, h)
+
+        copy_rows(0, 0)
+        round_pair(nc.vector.tensor_copy, 0, 1)
+        copy_rows(0, 1)
+        round_pair(nc.vector.tensor_copy, 0, 0)
+        nc.sync.dma_start(out=out_by_place[:, 0:2, :], in_=o_rows[0][:])
+        round_pair(nc.scalar.copy, 1, 0)
+        round_pair(nc.vector.tensor_copy, 1, 1)
+        for h in range(HALVES):
+            quantize(o_codes[:, columns(h, P)], o_scales[:, columns(h, P)], o_bf[h][:].rearrange("p q t -> p (q t)"))
+
+        queues = (nc.sync, nc.scalar)
         for h in range(HALVES):
             copy_rows(1, h)
-        nc.scalar.dma_start(out=out_dealt[:, 2:4, :], in_=o_rows[1][:])
+            queues[h].dma_start(out=out_by_place[:, 2:4, columns(h, P)], in_=o_rows[1][:, :, columns(h, P)])
         nc.sync.dma_start(out=out_1[0].rearrange("p c r -> p (c r)").bitcast(I32), in_=o_codes[:].bitcast(I32))
-        for quad in range(4):
-            queue = nc.sync if quad < 3 else nc.scalar
-            queue.dma_start(
-                out=out_2[0, 4 * quad : 4 * quad + 4, :].bitcast(I32),
+        for quad in range(QUADRANTS):
+            queues[quad // 2].dma_start(
+                out=out_2[0, columns(quad, 4), :].bitcast(I32),
                 in_=o_scales[32 * quad : 32 * quad + 4, :].bitcast(I32),
             )

from contextlib import ExitStack

import concourse.mybir as mybir
from concourse.masks import make_identity

D, T, I, Q, E = 512, 2048, 512, 256, 512
FLOPS = 2 * (2 * D * Q * I + I * E * Q)
BYTES = 4 * (2 * D * Q + T + I + E * T + E * Q) + D * T // 2 + D * T // 32 + 2 * 128 * I // 16 + E * Q + E * Q // 32

F32 = mybir.dt.float32
BF16 = mybir.dt.bfloat16
I32 = mybir.dt.int32
U32 = mybir.dt.uint32
U16 = mybir.dt.uint16
U8 = mybir.dt.uint8
FP8X4 = mybir.dt.float8_e4m3fn_x4
FP4X4 = mybir.dt.float4_e2m1fn_x4
ALU = mybir.AluOpType
ACT = mybir.ActivationFunctionType
AXIS = mybir.AxisListType

P = 128
PLACES = 4
BANK = 512
QUADRANTS = 4
SLOT_TILES = I // P
HALVES = Q // P
LIST_COLUMNS = I // 16
SHARE_ROW = P - 1
RUN = 4
SUMMED_BY_TENSOR = (0, 1)
SUMMED_BY_VECTOR = (2, 3)


def tile_attend_slotmixture_pl_kernel(
    tc, query, query2, keys_words, keys_scales, share, size, vals, offs, out_0, out_1, out_2
):
    nc = tc.nc
    with ExitStack() as ctx:
        sb = ctx.enter_context(tc.tile_pool(name="sb", bufs=1))
        ps = ctx.enter_context(tc.psum_pool(name="ps", bufs=1))

        def sbuf(name, shape, dtype, tag=None):
            return sb.tile(shape, dtype, name=name, tag=tag or name, align_bytes=64)

        def bank(index, name):
            return ps.tile([P, BANK], F32, name=name, tag=f"bank{index}")

        def columns(j, width):
            return slice(j * width, (j + 1) * width)

        def quantize(codes, scales, values):
            nc.vector.quantize_mx(out=codes.bitcast(FP8X4), scales=scales, in_=values)

        offsets = sbuf("offsets", [P, LIST_COLUMNS], U16)
        share_pool = sbuf("share_pool", [P, T], F32)
        key_scale_pool = sbuf("key_scale_pool", [P, T], U8)
        key_word_pool = sbuf("key_word_pool", [P, T], U16)
        q_raw = [sbuf(f"q_raw{j}", [P, PLACES * Q], F32) for j in range(2)]
        size_cols = sbuf("size_cols", [P, PLACES], F32)
        val_pool = [sbuf(f"val_pool{t}", [P, T], F32) for t in range(PLACES)]
        ident = sbuf("ident", [P, P], F32)
        zero = sbuf("zero", [P, 1], F32)
        one = sbuf("one", [P, 1], F32)

        nc.vector.memset(share_pool[0:SHARE_ROW, 0 : T // 2].bitcast(I32), 0)
        nc.gpsimd.memset(key_scale_pool[:].bitcast(I32), 0)
        nc.gpsimd.memset(zero[:], 0.0)
        nc.gpsimd.memset(share_pool[0:SHARE_ROW, T // 2 : T].bitcast(I32), 0)
        make_identity(nc, ident[:])

        nc.sync.dma_start(offsets[:], offs)
        nc.sync.dma_start(out=share_pool[SHARE_ROW:P, :], in_=share[SHARE_ROW:P, :])
        nc.sync.dma_start(out=q_raw[0][:], in_=query.rearrange("(p t) q -> p (t q)", t=PLACES))
        for quad in range(QUADRANTS):
            nc.sync.dma_start(
                out=key_scale_pool[32 * quad : 32 * quad + 4, :].bitcast(I32),
                in_=keys_scales[0, columns(quad, 4), :].bitcast(I32),
            )
        nc.scalar.activation(one[:], zero[:], ACT.Exp)
        nc.sync.dma_start(out=key_word_pool[:].bitcast(I32), in_=keys_words[0].bitcast(I32))
        nc.sync.dma_start(out=size_cols[:], in_=size.rearrange("o (p t) -> p (o t)", t=PLACES))
        nc.sync.dma_start(out=q_raw[1][:], in_=query2.rearrange("(p t) q -> p (t q)", t=PLACES))
        vals_by_place = vals.rearrange("(p t) c -> t p c", t=PLACES)
        for t in range(PLACES):
            nc.sync.dma_start(out=val_pool[t][:], in_=vals_by_place[t])

        share_listed = sbuf("share_listed", [P, I], F32)
        nc.vector.tensor_copy(share_listed[:], share_pool[:].indirect(offsets[:]))
        key_scales = sbuf("key_scales", [P, I], U8)
        nc.vector.tensor_copy(key_scales[:], key_scale_pool[:].indirect(offsets[:]))

        share_ps = bank(6, "share_ps")
        for c in range(SLOT_TILES):
            nc.tensor.transpose(share_ps[:, columns(c, P)], share_listed[:, columns(c, P)], ident[:])

        q_bf = [sbuf(f"q_bf{j}", [P, PLACES * Q], BF16) for j in range(2)]
        q_codes = [sbuf(f"q_codes{j}", [P, Q], U32) for j in range(2)]
        q_scales = [sbuf(f"q_scales{j}", [P, Q], U8) for j in range(2)]

        def interleave_query(j):
            nc.scalar.copy(
                out=q_bf[j][:].rearrange("p (c r t) -> p c t r", r=RUN, t=PLACES),
                in_=q_raw[j][:].rearrange("p (t c r) -> p c t r", r=RUN, t=PLACES),
            )

        interleave_query(0)
        factors = sbuf("factors", [P, 2 * SLOT_TILES], F32, tag="q_raw0")
        factor = [factors[:, columns(j, SLOT_TILES)] for j in range(2)]
        share_cols = share_ps[:, SHARE_ROW:BANK:P]
        nc.scalar.copy(out=factor[0], in_=share_cols)
        nc.scalar.activation(factor[1], share_cols, ACT.Identity, bias=one[:], scale=-1.0)

        size_ps = bank(7, "size_ps")
        for t in range(PLACES):
            u, e = divmod(t, 2)
            nc.tensor.transpose(
                size_ps[:, u * 2 * P + e : (u + 1) * 2 * P : 2], size_cols[:, t : t + 1].to_broadcast([P, P]), ident[:]
            )

        key_words = [sbuf(f"key_words{g}", [P, I // 2], U16) for g in range(2)]

        def gather_key_words(g):
            nc.vector.tensor_copy(key_words[g][:], key_word_pool[:].indirect(offsets[:, columns(g, LIST_COLUMNS // 2)]))

        gather_key_words(0)
        quantize(q_codes[0][:], q_scales[0][:], q_bf[0][:])
        gather_key_words(1)
        interleave_query(1)
        quantize(q_codes[1][:], q_scales[1][:], q_bf[1][:])

        product_codes = sbuf("product_codes", [P, E + Q], U32, tag="val_pool3")
        v_codes = [product_codes[:, columns(g, 2 * P)] for g in range(2)]
        w_codes = product_codes[:, E : E + Q]
        v_scales = [sbuf(f"v_scales{g}", [P, 2 * P], U8) for g in range(2)]
        v_listed = [sbuf(f"v_listed{t}", [P, I], BF16) for t in range(PLACES)]

        def gather_values(t):
            nc.vector.tensor_copy(v_listed[t][:], val_pool[t][:].indirect(offsets[:]))

        def turn_words(turned, runs, dst):
            for u in range(2):
                nc.tensor.transpose(turned[:, columns(u, P)], runs[u], ident[:])
            nc.scalar.copy(
                out=dst.bitcast(F32).rearrange("p (c u) -> p c u", u=2),
                in_=turned[:, 0 : 2 * P].rearrange("p (u c) -> p c u", u=2),
            )

        summed = sbuf("summed", [P, len(SUMMED_BY_VECTOR) * Q], F32, tag="val_pool0")
        a_scaled = sbuf("a_scaled", [P, SLOT_TILES * Q], F32, tag="q_raw1")
        part = {(0, c): a_scaled[:, columns(c, Q)] for c in range(SLOT_TILES)}
        for c in SUMMED_BY_TENSOR:
            part[1, c] = sbuf(f"b_scaled{c}", [P, Q], F32)[:]
        for n, c in enumerate(SUMMED_BY_VECTOR):
            part[1, c] = summed[:, columns(n, Q)]
        s_ps = [bank(4 + h, f"s_ps{h}") for h in range(HALVES)]

        def score(j, c, out):
            nc.tensor.matmul_mx(
                out=out,
                lhsT=key_words[c // 2][:, columns(c % 2, P)].bitcast(FP4X4),
                lhsT_scale=key_scales[:, columns(c, P)],
                rhs=q_codes[j][:].bitcast(FP8X4),
                rhs_scale=q_scales[j][:],
                start=True,
                stop=True,
            )

        def scale(j, c, sums):
            nc.scalar.activation(part[j, c], sums, ACT.Copy, scale=factor[j][:, c : c + 1])

        a_banks = [bank(b, f"a_ps{b}") for b in (0, 1, 2)]
        a_ps = [a_banks[0][:, 0:Q], a_banks[1][:, 0:Q], a_banks[2][:, 0:Q], a_banks[2][:, Q : 2 * Q]]
        for c in range(SLOT_TILES):
            score(0, c, a_ps[c])
        for c in range(SLOT_TILES):
            scale(0, c, a_ps[c])
        b_banks = [bank(b, f"b_ps{b}") for b in (3, 6, 0)]
        b_ps = [b_banks[2][:, 0:Q], b_banks[2][:, Q : 2 * Q], b_banks[0][:, 0:Q], b_banks[1][:, 0:Q]]
        for c in SUMMED_BY_VECTOR + SUMMED_BY_TENSOR:
            score(1, c, b_ps[c])
        for c in SUMMED_BY_TENSOR:
            scale(1, c, b_ps[c])
        gather_values(0)
        for c in SUMMED_BY_VECTOR:
            nc.vector.scalar_tensor_tensor(part[1, c], b_ps[c], factor[1][:, c : c + 1], part[0, c], ALU.mult, ALU.add)

        turns = [(0, c) for c in SUMMED_BY_TENSOR] + [(1, c) for c in range(SLOT_TILES)]
        for j, c in turns:
            for h in range(HALVES):
                nc.tensor.matmul(
                    s_ps[h][:, columns(c, P)],
                    part[j, c][:, columns(h, P)],
                    ident[:],
                    is_transpose=True,
                    start=((j, c) == turns[0]),
                    stop=((j, c) == turns[-1]),
                )

        gather_values(1)

        neg_max = sbuf("neg_max", [P, HALVES], F32, tag="val_pool1")
        row_sum = sbuf("row_sum", [P, HALVES], F32)
        inv_sum = sbuf("inv_sum", [P, HALVES], F32, tag="val_pool2")
        p_exp = [sbuf(f"p_exp{h}", [P, I], F32) for h in range(HALVES)]
        w_rows = [sbuf(f"w_rows{h}", [P, I], BF16) for h in range(HALVES)]
        w_bf = sbuf("w_bf", [P, PLACES * Q], BF16)
        w_scales = sbuf("w_scales", [P, Q], U8)
        for h in range(HALVES):
            nc.vector.tensor_reduce(neg_max[:, h : h + 1], s_ps[h][:], AXIS.X, ALU.max, negate=True)
            nc.scalar.activation(
                p_exp[h][:].rearrange("p (u s e) -> p u s e", u=2, e=2),
                s_ps[h][:].rearrange("p (s u e) -> p u s e", u=2, e=2),
                ACT.Exp,
                bias=neg_max[:, h : h + 1],
                scale=1.0,
                accum_out=row_sum[:, h : h + 1],
            )

        v_bf = [sbuf("v_bf0", [P, 2 * I], BF16, tag="val_pool1"), sbuf("v_bf1", [P, 2 * I], BF16)]

        def turn_values(t):
            words = v_listed[t][:].bitcast(F32)
            runs = [words[:, u : 2 * P : 2] for u in range(2)]
            turn_words(bank(t % 2, f"v_ps{t}"), runs, v_bf[t // 2][:, columns(t % 2, I)])

        turn_values(0)
        turn_values(1)
        gather_values(2)
        turn_values(2)
        nc.vector.reciprocal(inv_sum[:], row_sum[:])
        for h, free_bank in enumerate((6, 3)):
            nc.vector.scalar_tensor_tensor(w_rows[h][:], p_exp[h][:], inv_sum[:, h : h + 1], size_ps[:], ALU.mult, ALU.mult)
            words = w_rows[h][:].bitcast(F32)
            runs = [words[:, columns(u, P)] for u in range(2)]
            turn_words(bank(free_bank, f"w_ps{h}"), runs, w_bf[:, columns(h, I)])
        gather_values(3)
        turn_values(3)
        quantize(w_codes, w_scales[:], w_bf[:])
        quantize(v_codes[0], v_scales[0][:], v_bf[0][:])
        for e in range(2):
            quantize(v_codes[1][:, columns(e, P)], v_scales[1][:, columns(e, P)], v_bf[1][:, columns(e, I)])

        o_ps = [[bank(b, f"o_ps{b}") for b in free_banks] for free_banks in ((2, 6), (4, 5))]
        o_rows = [sbuf(f"o_rows{g}", [P, 2, Q], F32) for g in range(2)]
        o_bf = [sbuf(f"o_bf{h}", [P, P, PLACES], BF16) for h in range(HALVES)]
        o_codes = sbuf("o_codes", [P, Q], U32)
        o_scales = sbuf("o_scales", [P, Q], U8)
        out_by_place = out_0.rearrange("(p t) q -> p t q", t=PLACES)

        def multiply(g, e, h):
            nc.tensor.matmul_mx(
                out=o_ps[g][h][:, columns(e, P)],
                lhsT=v_codes[g][:, columns(e, P)].bitcast(FP8X4),
                lhsT_scale=v_scales[g][:, columns(e, P)],
                rhs=w_codes[:, columns(h, P)].bitcast(FP8X4),
                rhs_scale=w_scales[:, columns(h, P)],
                start=True,
                stop=True,
            )

        def copy_rows(g, h):
            nc.scalar.copy(
                out=o_rows[g][:, :, columns(h, P)],
                in_=o_ps[g][h][:, 0 : 2 * P].rearrange("p (e q) -> p e q", e=2),
            )

        def round_pair(copy, g, h):
            copy(
                out=o_bf[h][:, :, columns(g, 2)],
                in_=o_ps[g][h][:, 0 : 2 * P].rearrange("p (e q) -> p q e", e=2),
            )

        for h in range(HALVES):
            for e in range(2):
                multiply(0, e, h)
        for e in range(2):
            for h in range(HALVES):
                multiply(1, e, h)

        copy_rows(0, 0)
        round_pair(nc.vector.tensor_copy, 0, 1)
        copy_rows(0, 1)
        round_pair(nc.vector.tensor_copy, 0, 0)
        nc.sync.dma_start(out=out_by_place[:, 0:2, :], in_=o_rows[0][:])
        round_pair(nc.scalar.copy, 1, 0)
        round_pair(nc.vector.tensor_copy, 1, 1)
        for h in range(HALVES):
            quantize(o_codes[:, columns(h, P)], o_scales[:, columns(h, P)], o_bf[h][:].rearrange("p q t -> p (q t)"))

        queues = (nc.sync, nc.scalar)
        for h in range(HALVES):
            copy_rows(1, h)
            queues[h].dma_start(out=out_by_place[:, 2:4, columns(h, P)], in_=o_rows[1][:, :, columns(h, P)])
        nc.sync.dma_start(out=out_1[0].rearrange("p c r -> p (c r)").bitcast(I32), in_=o_codes[:].bitcast(I32))
        for quad in range(QUADRANTS):
            queues[quad // 2].dma_start(
                out=out_2[0, columns(quad, 4), :].bitcast(I32),
                in_=o_scales[32 * quad : 32 * quad + 4, :].bitcast(I32),
            )
